import numpy as np
import ml_dtypes


def mxq(x, axis, fmt="e4m3"):
    dtype, down = {"e4m3": (ml_dtypes.float8_e4m3fn, 7), "e5m2": (ml_dtypes.float8_e5m2, 14)}[fmt]
    v = np.moveaxis(np.asarray(x, np.float32).astype(ml_dtypes.bfloat16).astype(np.float64), axis, -1)
    blocks = v.reshape(v.shape[:-1] + (-1, 32))
    amax = np.abs(blocks).max(-1, keepdims=True)
    byte = np.maximum(np.where(amax > 0, np.frexp(amax)[1] - 1 + 127, 0) - down, 1)
    scale = np.exp2(byte - 127.0)
    codes = (blocks / scale).astype(np.float32).astype(dtype).astype(np.float64)
    return np.moveaxis((codes * scale).reshape(v.shape), -1, axis)


WIDE = False


def mx_kscale(k):
    if not WIDE:
        return np.ones(k)
    levels = np.array([10, -10, 5, -5, 0])
    if k % 512:
        return np.exp2(np.random.permutation(np.resize(levels, k // 32))).repeat(32)
    a = np.empty((k // 512, 16))
    for p in range(k // 512):
        a[p, :8] = np.random.permutation(np.resize(levels, 8))
        for g in range(8):
            far = levels[np.abs(levels - a[p, g]) >= 10]
            a[p, g + 8] = far[np.random.randint(len(far))]
    return np.exp2(a.ravel()).repeat(32)


def f64(x):
    return np.asarray(x).astype(np.float64)


def striped(idx):
    return np.tile(np.asarray(idx).reshape(-1, 16).T, (8, 1)).astype(np.uint16)


def unstriped(offs):
    return offs[:16].T.reshape(-1).astype(np.int64)


E2M1 = np.array([0.0, 0.5, 1.0, 1.5, 2.0, 3.0, 4.0, 6.0, -0.0, -0.5, -1.0, -1.5, -2.0, -3.0, -4.0, -6.0])


def pack_weight(w, fmt):
    k, n = w.shape
    w = f64(np.asarray(w, np.float32).astype(ml_dtypes.bfloat16)).reshape(k // 32, 32, n)
    amax = np.abs(w).max(1)
    if fmt == "e4m3":
        byte = np.frexp(amax)[1] - 1 + 127 - 7
    else:
        mant, ex = np.frexp(amax / 6.0)
        byte = np.where(mant > 0.5, ex, ex - 1) + 127
    byte = np.clip(np.where(amax > 0, byte, 1), 1, 254)
    scaled = (w * np.exp2(127.0 - byte)[:, None, :]).reshape(k, n).astype(np.float32)
    by_word = np.ascontiguousarray(scaled.reshape(k // 512, 128, 4, n).transpose(0, 1, 3, 2))
    if fmt == "e4m3":
        words = by_word.astype(ml_dtypes.float8_e4m3fn).view(np.uint8)
    else:
        c = by_word.astype(ml_dtypes.float4_e2m1fn).view(np.uint8) & 0xF
        words = (c[..., 0::2] | (c[..., 1::2] << 4)).reshape(k // 512, 128, 2 * n)
    return np.ascontiguousarray(words), np.ascontiguousarray(byte.astype(np.uint8).reshape(k // 512, 16, n))


def unpack_weight(words, scales, fmt):
    g, _, n = scales.shape
    words = np.ascontiguousarray(words).reshape(g, 128, n, -1)
    if fmt == "e4m3":
        vals = words.view(ml_dtypes.float8_e4m3fn).astype(np.float64)
    else:
        nib = np.empty((g, 128, n, 4), np.uint8)
        nib[..., 0::2] = words & 0xF
        nib[..., 1::2] = words >> 4
        vals = E2M1[nib]
    vals = vals * np.repeat(np.exp2(scales.astype(np.float64) - 127.0), 8, axis=1)[..., None]
    return vals.transpose(0, 1, 3, 2).reshape(g * 512, n)


B, N, T, D, NQ = 1, 1024, 4096, 512, 128
SEG = 64


def setup_inputs():
    n = np.random.standard_normal
    pages = np.random.permutation(T // 64)[:B * N // 64]
    idx = (pages[:, None] * 64 + np.arange(64)[None, :]).reshape(-1)
    s = mx_kscale(D)[:, None]
    kp = pack_weight(n((D, T)) / s, "e4m3")
    return {
        "qT": (n((B, D, NQ)) * s * (1.00 / np.sqrt(D))).astype(np.float32),
        "k_words": kp[0],
        "k_scales": kp[1],
        "offs": striped(idx),
    }


def reference(qT, k_words, k_scales, offs):
    idx = unstriped(offs)
    pick = lambda x, which: x[:, which].reshape(x.shape[0], B, -1).transpose(1, 0, 2)
    k = unpack_weight(k_words, k_scales, "e4m3")
    kg = pick(k, idx)
    qq = mxq(f64(qT), 1, "e4m3")
    a = qq.transpose(0, 2, 1) @ kg
    m = np.max(a, axis=-1, keepdims=True)
    x = a - m
    e = np.exp(x)
    l = np.sum(e, axis=-1, keepdims=True)
    y = (e / l * (np.log(l) - x)).reshape(B, NQ, N // SEG, SEG).sum(-1)
    return y

@@ -1,0 +1,152 @@
+from contextlib import ExitStack
+
+import concourse.mybir as mybir
+
+FLOPS = 134217728
+
+F32 = mybir.dt.float32
+BF16 = mybir.dt.bfloat16
+I32 = mybir.dt.int32
+U32 = mybir.dt.uint32
+U16 = mybir.dt.uint16
+U8 = mybir.dt.uint8
+FP8X4 = mybir.dt.float8_e4m3fn_x4
+ALU = mybir.AluOpType
+ACT = mybir.ActivationFunctionType
+AXIS_X = mybir.AxisListType.X
+
+P = 128
+PACK = 4
+POOL = 4096
+SLOTS = 1024
+HALF = 512
+PAGE = 64
+PAGES = SLOTS // PAGE
+HALF_PAGES = HALF // PAGE
+QUERIES = 128
+
+
+def tile_attend_page_ent_kernel(tc, qT, k_words, k_scales, offs, out):
+    nc = tc.nc
+    with ExitStack() as ctx:
+        keep = ctx.enter_context(tc.tile_pool(name="keep", bufs=1))
+        psum = ctx.enter_context(tc.psum_pool(name="psum", bufs=1))
+
+        offsets = keep.tile([P, SLOTS // 16], U16, name="offsets")
+        pool_words = keep.tile([P, POOL], U32, name="pool_words")
+        pool_scales = keep.tile([P, POOL], U8, name="pool_scales", tag="shared", align_bytes=64)
+        q_raw = keep.tile([P, PACK, QUERIES], F32, name="q_raw")
+
+        nc.vector.memset(pool_scales[:].bitcast(I32), 0)
+        nc.sync.dma_start(offsets[:], offs)
+        nc.sync.dma_start(q_raw[:], qT[0].rearrange("(p j) w -> p j w", j=PACK))
+        words_in = k_words[0].rearrange("p t r -> p (t r)").bitcast(I32)
+        nc.sync.dma_start(pool_words[:, : POOL // 2].bitcast(I32), words_in[:, : POOL // 2])
+        for quad in range(4):
+            nc.scalar.dma_start(
+                pool_scales[32 * quad : 32 * quad + 4, :].bitcast(I32),
+                k_scales[0, 4 * quad : 4 * quad + 4, :].bitcast(I32),
+            )
+        nc.scalar.dma_start(pool_words[:, POOL // 2 :].bitcast(I32), words_in[:, POOL // 2 :])
+
+        q_bf16 = keep.tile([P, QUERIES, PACK], BF16, name="q_bf16", align_bytes=64)
+        q_words = keep.tile([P, QUERIES], U32, name="q_words", align_bytes=64)
+        q_scales = keep.tile([P, QUERIES], U8, name="q_scales", align_bytes=64)
+        nc.scalar.copy(out=q_bf16[:], in_=q_raw[:].rearrange("p j w -> p w j"))
+        nc.vector.quantize_mx(
+            out=q_words[:].bitcast(FP8X4), scales=q_scales[:], in_=q_bf16[:].rearrange("p w j -> p (w j)")
+        )
+
+        key_scales = keep.tile([P, SLOTS], U8, name="key_scales", align_bytes=64)
+        nc.vector.tensor_copy(key_scales[:], pool_scales[:].indirect(offsets[:]))
+
+        scores = []
+        for h in range(2):
+            key_words = keep.tile([P, HALF], U32, name=f"key_words{h}", tag=("shared", "key_words1")[h], align_bytes=64)
+            cols = slice(h * HALF // 16, (h + 1) * HALF // 16)
+            nc.vector.tensor_copy(key_words[:], pool_words[:].indirect(offsets[:, cols]))
+            bank = psum.tile([P, HALF], F32, name=f"scores{h}")
+            nc.tensor.matmul_mx(
+                out=bank[:],
+                lhsT=q_words[:].bitcast(FP8X4),
+                lhsT_scale=q_scales[:],
+                rhs=key_words[:].bitcast(FP8X4),
+                rhs_scale=key_scales[:, h * HALF : (h + 1) * HALF],
+                start=True,
+                stop=True,
+            )
+            scores.append(bank)
+
+        neg_max = keep.tile([P, 2], F32, name="neg_max")
+        negated = keep.tile([P, HALF], F32, name="negated")
+        nc.vector.tensor_reduce(out=neg_max[:, 0:1], in_=scores[0][:], axis=AXIS_X, op=ALU.max, negate=True)
+        nc.vector.tensor_scalar(
+            out=negated[:], in0=scores[1][:], scalar1=-1.0, scalar2=neg_max[:, 0:1],
+            op0=ALU.mult, op1=ALU.min, accum_out=neg_max[:, 1:2],
+        )
+
+        terms = [keep.tile([P, 2, HALF], F32, name=f"terms{h}") for h in range(2)]
+        half_sum = keep.tile([P, 2], F32, name="half_sum")
+        shift = keep.tile([P, 1], F32, name="shift")
+        factor = keep.tile([P, 2], F32, name="factor")
+        nc.scalar.activation(
+            out=terms[0][:, 0, :], in_=scores[0][:], func=ACT.Exp, bias=neg_max[:, 0:1], accum_out=half_sum[:, 0:1]
+        )
+        nc.scalar.activation(
+            out=terms[1][:, 0, :], in_=scores[1][:], func=ACT.Exp, bias=neg_max[:, 1:2], accum_out=half_sum[:, 1:2]
+        )
+        nc.scalar.activation(out=factor[:], in_=neg_max[:], func=ACT.Exp, scale=-1.0, bias=neg_max[:, 1:2])
+        log_sum = keep.tile([P, 1], F32, name="log_sum")
+        nc.scalar.activation(
+            out=log_sum[:], in_=half_sum[:, 0:1], func=ACT.Ln, scale=factor[:, 0:1], bias=half_sum[:, 1:2]
+        )
+
+        sums = keep.tile([P, 2, PAGES], F32, name="sums")
+        row_sum = keep.tile([P, 1], F32, name="row_sum")
+        inverse = keep.tile([P, 1], F32, name="inverse")
+
+        def products(h):
+            nc.vector.scalar_tensor_tensor(
+                out=terms[h][:, 1, :], in0=scores[h][:], scalar=neg_max[:, h : h + 1], in1=terms[h][:, 0, :],
+                op0=ALU.add, op1=ALU.mult,
+            )
+
+        def page_sums(h, kind):
+            nc.vector.tensor_reduce(
+                out=sums[:, kind, h * HALF_PAGES : (h + 1) * HALF_PAGES],
+                in_=terms[h][:, kind, :].rearrange("p (j i) -> p j i", i=PAGE),
+                axis=AXIS_X,
+                op=ALU.add,
+            )
+
+        nc.vector.tensor_tensor(out=shift[:], in0=neg_max[:, 1:2], in1=neg_max[:, 0:1], op=ALU.subtract)
+        products(0)
+        page_sums(0, 0)
+        products(1)
+        page_sums(0, 1)
+        nc.vector.tensor_scalar(
+            out=row_sum[:], in0=half_sum[:, 0:1], scalar1=factor[:, 0:1], scalar2=half_sum[:, 1:2],
+            op0=ALU.mult, op1=ALU.add,
+        )
+        page_sums(1, 1)
+        nc.vector.reciprocal(out=inverse[:], in_=row_sum[:])
+        nc.vector.scalar_tensor_tensor(
+            out=sums[:, 1, 0:HALF_PAGES], in0=sums[:, 0, 0:HALF_PAGES], scalar=shift[:], in1=sums[:, 1, 0:HALF_PAGES],
+            op0=ALU.mult, op1=ALU.add,
+        )
+        page_sums(1, 0)
+
+        unscaled = keep.tile([P, PAGES], F32, name="unscaled")
+        result = keep.tile([P, PAGES], F32, name="result")
+        nc.vector.scalar_tensor_tensor(
+            out=unscaled[:], in0=sums[:, 0, :], scalar=log_sum[:], in1=sums[:, 1, :], op0=ALU.mult, op1=ALU.subtract
+        )
+        nc.vector.scalar_tensor_tensor(
+            out=result[:].rearrange("p (h j) -> p h j", h=2),
+            in0=unscaled[:].rearrange("p (h j) -> p h j", h=2),
+            scalar=inverse[:],
+            in1=factor[:].unsqueeze(2).to_broadcast([P, 2, HALF_PAGES]),
+            op0=ALU.mult,
+            op1=ALU.mult,
+        )
+        nc.sync.dma_start(out[0], result[:])

@@ -1,3 +1,4 @@
+import math
 from contextlib import ExitStack
 
 import concourse.mybir as mybir
@@ -24,6 +25,8 @@ PAGE = 64
 PAGES = SLOTS // PAGE
 HALF_PAGES = HALF // PAGE
 QUERIES = 128
+LN2_PER_BIT = math.log(2.0) / 2**23
+GUESS_BIAS = round(math.log(2.0) * (256 + 127 - 0.043) * 64) / 64
 
 
 def tile_attend_page_ent_kernel(tc, qT, k_words, k_scales, offs, out):
@@ -41,36 +44,36 @@ def tile_attend_page_ent_kernel(tc, qT, k_words, k_scales, offs, out):
         nc.sync.dma_start(offsets[:], offs)
         nc.sync.dma_start(q_raw[:], qT[0].rearrange("(p j) w -> p j w", j=PACK))
         words_in = k_words[0].rearrange("p t r -> p (t r)").bitcast(I32)
-        nc.sync.dma_start(pool_words[:, : POOL // 2].bitcast(I32), words_in[:, : POOL // 2])
+        nc.sync.dma_start(pool_words[:].bitcast(I32), words_in)
         for quad in range(4):
             nc.scalar.dma_start(
                 pool_scales[32 * quad : 32 * quad + 4, :].bitcast(I32),
                 k_scales[0, 4 * quad : 4 * quad + 4, :].bitcast(I32),
             )
-        nc.scalar.dma_start(pool_words[:, POOL // 2 :].bitcast(I32), words_in[:, POOL // 2 :])
 
-        q_bf16 = keep.tile([P, QUERIES, PACK], BF16, name="q_bf16", align_bytes=64)
+        q_bf16 = keep.tile([P, QUERIES, PACK], BF16, name="q_bf16", tag="shared_q", align_bytes=64)
         q_words = keep.tile([P, QUERIES], U32, name="q_words", align_bytes=64)
         q_scales = keep.tile([P, QUERIES], U8, name="q_scales", align_bytes=64)
-        nc.scalar.copy(out=q_bf16[:], in_=q_raw[:].rearrange("p j w -> p w j"))
+        nc.vector.tensor_copy(out=q_bf16[:], in_=q_raw[:].rearrange("p j w -> p w j"))
         nc.vector.quantize_mx(
             out=q_words[:].bitcast(FP8X4), scales=q_scales[:], in_=q_bf16[:].rearrange("p w j -> p (w j)")
         )
 
-        key_scales = keep.tile([P, SLOTS], U8, name="key_scales", align_bytes=64)
+        key_scales = keep.tile([P, SLOTS], U8, name="key_scales", tag="shared_q", align_bytes=64)
         nc.vector.tensor_copy(key_scales[:], pool_scales[:].indirect(offsets[:]))
 
         scores = []
+        key_words = keep.tile([P, SLOTS], U32, name="key_words", tag="shared", align_bytes=64)
         for h in range(2):
-            key_words = keep.tile([P, HALF], U32, name=f"key_words{h}", tag=("shared", "key_words1")[h], align_bytes=64)
+            slots = slice(h * HALF, (h + 1) * HALF)
             cols = slice(h * HALF // 16, (h + 1) * HALF // 16)
-            nc.vector.tensor_copy(key_words[:], pool_words[:].indirect(offsets[:, cols]))
+            nc.vector.tensor_copy(key_words[:, slots], pool_words[:].indirect(offsets[:, cols]))
             bank = psum.tile([P, HALF], F32, name=f"scores{h}")
             nc.tensor.matmul_mx(
                 out=bank[:],
                 lhsT=q_words[:].bitcast(FP8X4),
                 lhsT_scale=q_scales[:],
-                rhs=key_words[:].bitcast(FP8X4),
+                rhs=key_words[:, slots].bitcast(FP8X4),
                 rhs_scale=key_scales[:, h * HALF : (h + 1) * HALF],
                 start=True,
                 stop=True,
@@ -78,75 +81,88 @@ def tile_attend_page_ent_kernel(tc, qT, k_words, k_scales, offs, out):
             scores.append(bank)
 
         neg_max = keep.tile([P, 2], F32, name="neg_max")
-        negated = keep.tile([P, HALF], F32, name="negated")
-        nc.vector.tensor_reduce(out=neg_max[:, 0:1], in_=scores[0][:], axis=AXIS_X, op=ALU.max, negate=True)
-        nc.vector.tensor_scalar(
-            out=negated[:], in0=scores[1][:], scalar1=-1.0, scalar2=neg_max[:, 0:1],
-            op0=ALU.mult, op1=ALU.min, accum_out=neg_max[:, 1:2],
-        )
+        neg_scores = [keep.tile([P, HALF], F32, name=f"neg_scores{h}") for h in range(2)]
+        for h in range(2):
+            nc.vector.tensor_scalar(
+                out=neg_scores[h][:], in0=scores[h][:], scalar1=-1.0, scalar2=neg_max[:, 0:1] if h else None,
+                op0=ALU.mult, op1=ALU.min, accum_out=neg_max[:, h : h + 1],
+            )
 
-        terms = [keep.tile([P, 2, HALF], F32, name=f"terms{h}") for h in range(2)]
-        half_sum = keep.tile([P, 2], F32, name="half_sum")
-        shift = keep.tile([P, 1], F32, name="shift")
+        exps = keep.tile([P, SLOTS], F32, name="exps")
+        weighted = keep.tile([P, SLOTS], F32, name="weighted")
+        exp_sums = keep.tile([P, PAGES + 1], F32, name="exp_sums")
+        weighted_sums = keep.tile([P, PAGES], F32, name="weighted_sums")
         factor = keep.tile([P, 2], F32, name="factor")
-        nc.scalar.activation(
-            out=terms[0][:, 0, :], in_=scores[0][:], func=ACT.Exp, bias=neg_max[:, 0:1], accum_out=half_sum[:, 0:1]
-        )
-        nc.scalar.activation(
-            out=terms[1][:, 0, :], in_=scores[1][:], func=ACT.Exp, bias=neg_max[:, 1:2], accum_out=half_sum[:, 1:2]
-        )
-        nc.scalar.activation(out=factor[:], in_=neg_max[:], func=ACT.Exp, scale=-1.0, bias=neg_max[:, 1:2])
-        log_sum = keep.tile([P, 1], F32, name="log_sum")
-        nc.scalar.activation(
-            out=log_sum[:], in_=half_sum[:, 0:1], func=ACT.Ln, scale=factor[:, 0:1], bias=half_sum[:, 1:2]
-        )
+        spare = keep.tile([P, HALF_PAGES + 1], F32, name="spare")
 
-        sums = keep.tile([P, 2, PAGES], F32, name="sums")
-        row_sum = keep.tile([P, 1], F32, name="row_sum")
-        inverse = keep.tile([P, 1], F32, name="inverse")
+        def page_exp(page):
+            h, j = divmod(page, HALF_PAGES)
+            nc.scalar.activation(
+                out=exps[:, page * PAGE : (page + 1) * PAGE], in_=neg_scores[h][:, j * PAGE : (j + 1) * PAGE],
+                func=ACT.Exp, scale=-1.0, bias=neg_max[:, h : h + 1], accum_out=exp_sums[:, page : page + 1],
+            )
 
-        def products(h):
+        def page_weighted(page):
+            h, j = divmod(page, HALF_PAGES)
             nc.vector.scalar_tensor_tensor(
-                out=terms[h][:, 1, :], in0=scores[h][:], scalar=neg_max[:, h : h + 1], in1=terms[h][:, 0, :],
-                op0=ALU.add, op1=ALU.mult,
+                out=weighted[:, page * PAGE : (page + 1) * PAGE], in0=neg_scores[h][:, j * PAGE : (j + 1) * PAGE],
+                scalar=neg_max[:, 1:2], in1=exps[:, page * PAGE : (page + 1) * PAGE],
+                op0=ALU.subtract, op1=ALU.mult, accum_out=weighted_sums[:, page : page + 1],
             )
 
-        def page_sums(h, kind):
-            nc.vector.tensor_reduce(
-                out=sums[:, kind, h * HALF_PAGES : (h + 1) * HALF_PAGES],
-                in_=terms[h][:, kind, :].rearrange("p (j i) -> p j i", i=PAGE),
-                axis=AXIS_X,
-                op=ALU.add,
-            )
-
-        nc.vector.tensor_tensor(out=shift[:], in0=neg_max[:, 1:2], in1=neg_max[:, 0:1], op=ALU.subtract)
-        products(0)
-        page_sums(0, 0)
-        products(1)
-        page_sums(0, 1)
-        nc.vector.tensor_scalar(
-            out=row_sum[:], in0=half_sum[:, 0:1], scalar1=factor[:, 0:1], scalar2=half_sum[:, 1:2],
-            op0=ALU.mult, op1=ALU.add,
+        for page in range(HALF_PAGES):
+            page_exp(page)
+        nc.scalar.activation(out=factor[:], in_=neg_max[:], func=ACT.Exp, scale=-1.0, bias=neg_max[:, 1:2])
+        page_exp(HALF_PAGES)
+        page_exp(HALF_PAGES + 1)
+        nc.scalar.activation(
+            out=spare[:, :HALF_PAGES], in_=exp_sums[:, :HALF_PAGES], func=ACT.Identity, scale=factor[:, 0:1],
+            accum_out=exp_sums[:, PAGES : PAGES + 1],
         )
-        page_sums(1, 1)
-        nc.vector.reciprocal(out=inverse[:], in_=row_sum[:])
-        nc.vector.scalar_tensor_tensor(
-            out=sums[:, 1, 0:HALF_PAGES], in0=sums[:, 0, 0:HALF_PAGES], scalar=shift[:], in1=sums[:, 1, 0:HALF_PAGES],
-            op0=ALU.mult, op1=ALU.add,
-        )
-        page_sums(1, 0)
+        for page in range(HALF_PAGES + 2, PAGES):
+            page_exp(page)
 
-        unscaled = keep.tile([P, PAGES], F32, name="unscaled")
+        neg_sum = keep.tile([P, 1], F32, name="neg_sum")
+        nc.scalar.activation(
+            out=spare[:], in_=exp_sums[:, HALF_PAGES:], func=ACT.Identity, scale=-1.0, accum_out=neg_sum[:]
+        )
+        bits = neg_sum[:].bitcast(U32)
+        steps = keep.tile([P, 10], F32, name="steps")
+        t0, b0, c0, t1, b1, d1, t2, h2, sq, neg_log = [steps[:, i : i + 1] for i in range(10)]
+        nc.scalar.activation(out=t0, in_=bits, func=ACT.Exp, scale=-LN2_PER_BIT, bias=GUESS_BIAS)
+        nc.scalar.activation(out=b0, in_=bits, func=ACT.Identity, scale=-LN2_PER_BIT, bias=GUESS_BIAS + 1.0)
+        nc.scalar.activation(out=c0, in_=bits, func=ACT.Identity, scale=-LN2_PER_BIT, bias=GUESS_BIAS + 2.0)
+        nc.scalar.activation(out=t1, in_=t0, func=ACT.Exp, scale=neg_sum[:], bias=b0)
+        nc.scalar.activation(out=b1, in_=t0, func=ACT.Identity, scale=neg_sum[:], bias=c0)
+        nc.scalar.activation(out=t2, in_=t1, func=ACT.Exp, scale=neg_sum[:], bias=b1)
+        nc.scalar.activation(out=d1, in_=b1, func=ACT.Identity, bias=-0.5)
+        nc.scalar.activation(out=sq, in_=t2, func=ACT.Square, scale=neg_sum[:], bias=2.0)
+        nc.scalar.activation(out=h2, in_=t1, func=ACT.Identity, scale=neg_sum[:], bias=d1)
+        nc.scalar.activation(out=neg_log, in_=sq, func=ACT.Identity, scale=0.5, bias=h2)
+
+        neg_inverse = keep.tile([P, 1], F32, name="neg_inverse")
+        scaled_exp = keep.tile([P, PAGES], F32, name="scaled_exp")
+        scaled_weighted = keep.tile([P, PAGES], F32, name="scaled_weighted")
         result = keep.tile([P, PAGES], F32, name="result")
+
+        def normalise(dst, src):
+            nc.vector.scalar_tensor_tensor(
+                out=dst.rearrange("p (h j) -> p h j", h=2),
+                in0=src.rearrange("p (h j) -> p h j", h=2),
+                scalar=neg_inverse[:],
+                in1=factor[:].unsqueeze(2).to_broadcast([P, 2, HALF_PAGES]),
+                op0=ALU.mult,
+                op1=ALU.mult,
+            )
+
+        for page in range(PAGES):
+            page_weighted(page)
+            if page == 11:
+                nc.vector.reciprocal(out=neg_inverse[:], in_=neg_sum[:])
+            if page == 13:
+                normalise(scaled_exp[:], exp_sums[:, :PAGES])
+        normalise(scaled_weighted[:], weighted_sums[:])
         nc.vector.scalar_tensor_tensor(
-            out=unscaled[:], in0=sums[:, 0, :], scalar=log_sum[:], in1=sums[:, 1, :], op0=ALU.mult, op1=ALU.subtract
-        )
-        nc.vector.scalar_tensor_tensor(
-            out=result[:].rearrange("p (h j) -> p h j", h=2),
-            in0=unscaled[:].rearrange("p (h j) -> p h j", h=2),
-            scalar=inverse[:],
-            in1=factor[:].unsqueeze(2).to_broadcast([P, 2, HALF_PAGES]),
-            op0=ALU.mult,
-            op1=ALU.mult,
+            out=result[:], in0=scaled_exp[:], scalar=neg_log, in1=scaled_weighted[:], op0=ALU.mult, op1=ALU.subtract
         )
         nc.sync.dma_start(out[0], result[:])

@@ -25,6 +25,7 @@ PAGE = 64
 PAGES = SLOTS // PAGE
 HALF_PAGES = HALF // PAGE
 QUERIES = 128
+FIRST_ROW = P - 16
 LN2_PER_BIT = math.log(2.0) / 2**23
 GUESS_BIAS = round(math.log(2.0) * (256 + 127 - 0.043) * 64) / 64
 
@@ -40,27 +41,29 @@ def tile_attend_page_ent_kernel(tc, qT, k_words, k_scales, offs, out):
         pool_scales = keep.tile([P, POOL], U8, name="pool_scales", tag="shared", align_bytes=64)
         q_raw = keep.tile([P, PACK, QUERIES], F32, name="q_raw")
 
-        nc.vector.memset(pool_scales[:].bitcast(I32), 0)
+        key_scales = keep.tile([P, SLOTS], U8, name="key_scales", align_bytes=64)
         nc.sync.dma_start(offsets[:], offs)
+        nc.sync.dma_start(pool_scales[FIRST_ROW:, :].bitcast(I32), k_scales[0].bitcast(I32))
         nc.sync.dma_start(q_raw[:], qT[0].rearrange("(p j) w -> p j w", j=PACK))
-        words_in = k_words[0].rearrange("p t r -> p (t r)").bitcast(I32)
-        nc.sync.dma_start(pool_words[:].bitcast(I32), words_in)
+        nc.sync.dma_start(pool_words[:].bitcast(I32), k_words[0].rearrange("p t r -> p (t r)").bitcast(I32))
+        nc.vector.memset(pool_scales[:FIRST_ROW, :].bitcast(I32), 0)
+        nc.vector.memset(key_scales[:].bitcast(I32), 0)
+
+        listed_scales = keep.tile([P, SLOTS], U8, name="listed_scales")
+        nc.vector.tensor_copy(listed_scales[:], pool_scales[:].indirect(offsets[:]))
         for quad in range(4):
+            rows = slice(FIRST_ROW + 4 * quad, FIRST_ROW + 4 * quad + 4)
             nc.scalar.dma_start(
-                pool_scales[32 * quad : 32 * quad + 4, :].bitcast(I32),
-                k_scales[0, 4 * quad : 4 * quad + 4, :].bitcast(I32),
+                key_scales[32 * quad : 32 * quad + 4, :].bitcast(I32), listed_scales[rows, :].bitcast(I32)
             )
 
-        q_bf16 = keep.tile([P, QUERIES, PACK], BF16, name="q_bf16", tag="shared_q", align_bytes=64)
+        q_bf16 = keep.tile([P, QUERIES, PACK], BF16, name="q_bf16", tag="shared", align_bytes=64)
         q_words = keep.tile([P, QUERIES], U32, name="q_words", align_bytes=64)
         q_scales = keep.tile([P, QUERIES], U8, name="q_scales", align_bytes=64)
         nc.vector.tensor_copy(out=q_bf16[:], in_=q_raw[:].rearrange("p j w -> p w j"))
         nc.vector.quantize_mx(
             out=q_words[:].bitcast(FP8X4), scales=q_scales[:], in_=q_bf16[:].rearrange("p w j -> p (w j)")
         )
-
-        key_scales = keep.tile([P, SLOTS], U8, name="key_scales", tag="shared_q", align_bytes=64)
-        nc.vector.tensor_copy(key_scales[:], pool_scales[:].indirect(offsets[:]))
 
         scores = []
         key_words = keep.tile([P, SLOTS], U32, name="key_words", tag="shared", align_bytes=64)

@@ -14,7 +14,6 @@ U8 = mybir.dt.uint8
 FP8X4 = mybir.dt.float8_e4m3fn_x4
 ALU = mybir.AluOpType
 ACT = mybir.ActivationFunctionType
-AXIS_X = mybir.AxisListType.X
 
 P = 128
 PACK = 4
@@ -25,9 +24,16 @@ PAGE = 64
 PAGES = SLOTS // PAGE
 HALF_PAGES = HALF // PAGE
 QUERIES = 128
-FIRST_ROW = P - 16
+LIST_ROWS = 16
+SCALE_ROWS = 16
+FIRST_SCALE_ROW = P - SCALE_ROWS
+
 LN2_PER_BIT = math.log(2.0) / 2**23
 GUESS_BIAS = round(math.log(2.0) * (256 + 127 - 0.043) * 64) / 64
+
+RESCALE_BEFORE_PAGE = HALF_PAGES + 2
+RECIPROCAL_AFTER_PAGE = 11
+NORMALISE_AFTER_PAGE = 13
 
 
 def tile_attend_page_ent_kernel(tc, qT, k_words, k_scales, offs, out):
@@ -36,23 +42,23 @@ def tile_attend_page_ent_kernel(tc, qT, k_words, k_scales, offs, out):
         keep = ctx.enter_context(tc.tile_pool(name="keep", bufs=1))
         psum = ctx.enter_context(tc.psum_pool(name="psum", bufs=1))
 
-        offsets = keep.tile([P, SLOTS // 16], U16, name="offsets")
+        offsets = keep.tile([P, SLOTS // LIST_ROWS], U16, name="offsets")
         pool_words = keep.tile([P, POOL], U32, name="pool_words")
         pool_scales = keep.tile([P, POOL], U8, name="pool_scales", tag="shared", align_bytes=64)
         q_raw = keep.tile([P, PACK, QUERIES], F32, name="q_raw")
-
         key_scales = keep.tile([P, SLOTS], U8, name="key_scales", align_bytes=64)
+
         nc.sync.dma_start(offsets[:], offs)
-        nc.sync.dma_start(pool_scales[FIRST_ROW:, :].bitcast(I32), k_scales[0].bitcast(I32))
+        nc.sync.dma_start(pool_scales[FIRST_SCALE_ROW:, :].bitcast(I32), k_scales[0].bitcast(I32))
         nc.sync.dma_start(q_raw[:], qT[0].rearrange("(p j) w -> p j w", j=PACK))
         nc.sync.dma_start(pool_words[:].bitcast(I32), k_words[0].rearrange("p t r -> p (t r)").bitcast(I32))
-        nc.vector.memset(pool_scales[:FIRST_ROW, :].bitcast(I32), 0)
+        nc.vector.memset(pool_scales[:FIRST_SCALE_ROW, :].bitcast(I32), 0)
         nc.vector.memset(key_scales[:].bitcast(I32), 0)
 
         listed_scales = keep.tile([P, SLOTS], U8, name="listed_scales")
         nc.vector.tensor_copy(listed_scales[:], pool_scales[:].indirect(offsets[:]))
         for quad in range(4):
-            rows = slice(FIRST_ROW + 4 * quad, FIRST_ROW + 4 * quad + 4)
+            rows = slice(FIRST_SCALE_ROW + 4 * quad, FIRST_SCALE_ROW + 4 * quad + 4)
             nc.scalar.dma_start(
                 key_scales[32 * quad : 32 * quad + 4, :].bitcast(I32), listed_scales[rows, :].bitcast(I32)
             )
@@ -69,15 +75,15 @@ def tile_attend_page_ent_kernel(tc, qT, k_words, k_scales, offs, out):
         key_words = keep.tile([P, SLOTS], U32, name="key_words", tag="shared", align_bytes=64)
         for h in range(2):
             slots = slice(h * HALF, (h + 1) * HALF)
-            cols = slice(h * HALF // 16, (h + 1) * HALF // 16)
-            nc.vector.tensor_copy(key_words[:, slots], pool_words[:].indirect(offsets[:, cols]))
+            entries = slice(h * HALF // LIST_ROWS, (h + 1) * HALF // LIST_ROWS)
+            nc.vector.tensor_copy(key_words[:, slots], pool_words[:].indirect(offsets[:, entries]))
             bank = psum.tile([P, HALF], F32, name=f"scores{h}")
             nc.tensor.matmul_mx(
                 out=bank[:],
                 lhsT=q_words[:].bitcast(FP8X4),
                 lhsT_scale=q_scales[:],
                 rhs=key_words[:, slots].bitcast(FP8X4),
-                rhs_scale=key_scales[:, h * HALF : (h + 1) * HALF],
+                rhs_scale=key_scales[:, slots],
                 start=True,
                 stop=True,
             )
@@ -94,54 +100,47 @@ def tile_attend_page_ent_kernel(tc, qT, k_words, k_scales, offs, out):
         exps = keep.tile([P, SLOTS], F32, name="exps")
         weighted = keep.tile([P, SLOTS], F32, name="weighted")
         exp_sums = keep.tile([P, PAGES + 1], F32, name="exp_sums")
-        weighted_sums = keep.tile([P, PAGES], F32, name="weighted_sums")
+        neg_weighted_sums = keep.tile([P, PAGES], F32, name="neg_weighted_sums")
         factor = keep.tile([P, 2], F32, name="factor")
-        spare = keep.tile([P, HALF_PAGES + 1], F32, name="spare")
+        sum_terms = keep.tile([P, HALF_PAGES + 1], F32, name="sum_terms")
 
-        def page_exp(page):
+        for page in range(PAGES):
             h, j = divmod(page, HALF_PAGES)
+            if page == HALF_PAGES:
+                nc.scalar.activation(out=factor[:], in_=neg_max[:], func=ACT.Exp, scale=-1.0, bias=neg_max[:, 1:2])
+            if page == RESCALE_BEFORE_PAGE:
+                nc.scalar.activation(
+                    out=sum_terms[:, :HALF_PAGES], in_=exp_sums[:, :HALF_PAGES], func=ACT.Identity,
+                    scale=factor[:, 0:1], accum_out=exp_sums[:, PAGES : PAGES + 1],
+                )
             nc.scalar.activation(
                 out=exps[:, page * PAGE : (page + 1) * PAGE], in_=neg_scores[h][:, j * PAGE : (j + 1) * PAGE],
                 func=ACT.Exp, scale=-1.0, bias=neg_max[:, h : h + 1], accum_out=exp_sums[:, page : page + 1],
             )
 
-        def page_weighted(page):
-            h, j = divmod(page, HALF_PAGES)
-            nc.vector.scalar_tensor_tensor(
-                out=weighted[:, page * PAGE : (page + 1) * PAGE], in0=neg_scores[h][:, j * PAGE : (j + 1) * PAGE],
-                scalar=neg_max[:, 1:2], in1=exps[:, page * PAGE : (page + 1) * PAGE],
-                op0=ALU.subtract, op1=ALU.mult, accum_out=weighted_sums[:, page : page + 1],
-            )
-
-        for page in range(HALF_PAGES):
-            page_exp(page)
-        nc.scalar.activation(out=factor[:], in_=neg_max[:], func=ACT.Exp, scale=-1.0, bias=neg_max[:, 1:2])
-        page_exp(HALF_PAGES)
-        page_exp(HALF_PAGES + 1)
-        nc.scalar.activation(
-            out=spare[:, :HALF_PAGES], in_=exp_sums[:, :HALF_PAGES], func=ACT.Identity, scale=factor[:, 0:1],
-            accum_out=exp_sums[:, PAGES : PAGES + 1],
-        )
-        for page in range(HALF_PAGES + 2, PAGES):
-            page_exp(page)
-
         neg_sum = keep.tile([P, 1], F32, name="neg_sum")
         nc.scalar.activation(
-            out=spare[:], in_=exp_sums[:, HALF_PAGES:], func=ACT.Identity, scale=-1.0, accum_out=neg_sum[:]
+            out=sum_terms[:], in_=exp_sums[:, HALF_PAGES:], func=ACT.Identity, scale=-1.0, accum_out=neg_sum[:]
         )
+
         bits = neg_sum[:].bitcast(U32)
+        multiples = keep.tile([P, 2], F32, name="multiples")
+        nc.gpsimd.memset(multiples[:, 0:1], 2.0)
+        nc.gpsimd.memset(multiples[:, 1:2], 0.5)
         steps = keep.tile([P, 10], F32, name="steps")
-        t0, b0, c0, t1, b1, d1, t2, h2, sq, neg_log = [steps[:, i : i + 1] for i in range(10)]
-        nc.scalar.activation(out=t0, in_=bits, func=ACT.Exp, scale=-LN2_PER_BIT, bias=GUESS_BIAS)
-        nc.scalar.activation(out=b0, in_=bits, func=ACT.Identity, scale=-LN2_PER_BIT, bias=GUESS_BIAS + 1.0)
-        nc.scalar.activation(out=c0, in_=bits, func=ACT.Identity, scale=-LN2_PER_BIT, bias=GUESS_BIAS + 2.0)
-        nc.scalar.activation(out=t1, in_=t0, func=ACT.Exp, scale=neg_sum[:], bias=b0)
-        nc.scalar.activation(out=b1, in_=t0, func=ACT.Identity, scale=neg_sum[:], bias=c0)
-        nc.scalar.activation(out=t2, in_=t1, func=ACT.Exp, scale=neg_sum[:], bias=b1)
-        nc.scalar.activation(out=d1, in_=b1, func=ACT.Identity, bias=-0.5)
-        nc.scalar.activation(out=sq, in_=t2, func=ACT.Square, scale=neg_sum[:], bias=2.0)
-        nc.scalar.activation(out=h2, in_=t1, func=ACT.Identity, scale=neg_sum[:], bias=d1)
-        nc.scalar.activation(out=neg_log, in_=sq, func=ACT.Identity, scale=0.5, bias=h2)
+        exp0, bias_exp1, bias_line0, exp1, bias_line1, twice, halved, curve, line, neg_log = [
+            steps[:, i : i + 1] for i in range(10)
+        ]
+        twice_and_halved = steps[:, 5:7]
+        nc.scalar.activation(out=exp0, in_=bits, func=ACT.Exp, scale=-LN2_PER_BIT, bias=GUESS_BIAS)
+        nc.scalar.activation(out=bias_exp1, in_=bits, func=ACT.Identity, scale=-LN2_PER_BIT, bias=GUESS_BIAS + 1.0)
+        nc.scalar.activation(out=bias_line0, in_=bits, func=ACT.Identity, scale=-LN2_PER_BIT, bias=GUESS_BIAS + 1.25)
+        nc.scalar.activation(out=twice_and_halved, in_=multiples[:], func=ACT.Identity, scale=neg_sum[:])
+        nc.scalar.activation(out=exp1, in_=exp0, func=ACT.Exp, scale=neg_sum[:], bias=bias_exp1)
+        nc.scalar.activation(out=bias_line1, in_=exp0, func=ACT.Identity, scale=neg_sum[:], bias=bias_line0)
+        nc.scalar.activation(out=curve, in_=exp1, func=ACT.Exp, scale=twice, bias=2.0)
+        nc.scalar.activation(out=line, in_=exp1, func=ACT.Identity, scale=halved, bias=bias_line1)
+        nc.scalar.activation(out=neg_log, in_=curve, func=ACT.Identity, scale=0.25, bias=line)
 
         neg_inverse = keep.tile([P, 1], F32, name="neg_inverse")
         scaled_exp = keep.tile([P, PAGES], F32, name="scaled_exp")
@@ -159,12 +158,17 @@ def tile_attend_page_ent_kernel(tc, qT, k_words, k_scales, offs, out):
             )
 
         for page in range(PAGES):
-            page_weighted(page)
-            if page == 11:
+            h, j = divmod(page, HALF_PAGES)
+            nc.vector.scalar_tensor_tensor(
+                out=weighted[:, page * PAGE : (page + 1) * PAGE], in0=neg_scores[h][:, j * PAGE : (j + 1) * PAGE],
+                scalar=neg_max[:, 1:2], in1=exps[:, page * PAGE : (page + 1) * PAGE],
+                op0=ALU.subtract, op1=ALU.mult, accum_out=neg_weighted_sums[:, page : page + 1],
+            )
+            if page == RECIPROCAL_AFTER_PAGE:
                 nc.vector.reciprocal(out=neg_inverse[:], in_=neg_sum[:])
-            if page == 13:
+            if page == NORMALISE_AFTER_PAGE:
                 normalise(scaled_exp[:], exp_sums[:, :PAGES])
-        normalise(scaled_weighted[:], weighted_sums[:])
+        normalise(scaled_weighted[:], neg_weighted_sums[:])
         nc.vector.scalar_tensor_tensor(
             out=result[:], in0=scaled_exp[:], scalar=neg_log, in1=scaled_weighted[:], op0=ALU.mult, op1=ALU.subtract
         )

import math
from contextlib import ExitStack

import concourse.mybir as mybir

FLOPS = 134217728

F32 = mybir.dt.float32
BF16 = mybir.dt.bfloat16
I32 = mybir.dt.int32
U32 = mybir.dt.uint32
U16 = mybir.dt.uint16
U8 = mybir.dt.uint8
FP8X4 = mybir.dt.float8_e4m3fn_x4
ALU = mybir.AluOpType
ACT = mybir.ActivationFunctionType

P = 128
PACK = 4
POOL = 4096
SLOTS = 1024
HALF = 512
PAGE = 64
PAGES = SLOTS // PAGE
HALF_PAGES = HALF // PAGE
QUERIES = 128
LIST_ROWS = 16
SCALE_ROWS = 16
FIRST_SCALE_ROW = P - SCALE_ROWS

LN2_PER_BIT = math.log(2.0) / 2**23
GUESS_BIAS = round(math.log(2.0) * (256 + 127 - 0.043) * 64) / 64

RESCALE_BEFORE_PAGE = HALF_PAGES + 2
RECIPROCAL_AFTER_PAGE = 11
NORMALISE_AFTER_PAGE = 13


def tile_attend_page_ent_kernel(tc, qT, k_words, k_scales, offs, out):
    nc = tc.nc
    with ExitStack() as ctx:
        keep = ctx.enter_context(tc.tile_pool(name="keep", bufs=1))
        psum = ctx.enter_context(tc.psum_pool(name="psum", bufs=1))

        offsets = keep.tile([P, SLOTS // LIST_ROWS], U16, name="offsets")
        pool_words = keep.tile([P, POOL], U32, name="pool_words")
        pool_scales = keep.tile([P, POOL], U8, name="pool_scales", tag="shared", align_bytes=64)
        q_raw = keep.tile([P, PACK, QUERIES], F32, name="q_raw")
        key_scales = keep.tile([P, SLOTS], U8, name="key_scales", align_bytes=64)

        nc.sync.dma_start(offsets[:], offs)
        nc.sync.dma_start(pool_scales[FIRST_SCALE_ROW:, :].bitcast(I32), k_scales[0].bitcast(I32))
        nc.sync.dma_start(q_raw[:], qT[0].rearrange("(p j) w -> p j w", j=PACK))
        nc.sync.dma_start(pool_words[:].bitcast(I32), k_words[0].rearrange("p t r -> p (t r)").bitcast(I32))
        nc.vector.memset(pool_scales[:FIRST_SCALE_ROW, :].bitcast(I32), 0)
        nc.vector.memset(key_scales[:].bitcast(I32), 0)

        listed_scales = keep.tile([P, SLOTS], U8, name="listed_scales")
        nc.vector.tensor_copy(listed_scales[:], pool_scales[:].indirect(offsets[:]))
        for quad in range(4):
            rows = slice(FIRST_SCALE_ROW + 4 * quad, FIRST_SCALE_ROW + 4 * quad + 4)
            nc.scalar.dma_start(
                key_scales[32 * quad : 32 * quad + 4, :].bitcast(I32), listed_scales[rows, :].bitcast(I32)
            )

        q_bf16 = keep.tile([P, QUERIES, PACK], BF16, name="q_bf16", tag="shared", align_bytes=64)
        q_words = keep.tile([P, QUERIES], U32, name="q_words", align_bytes=64)
        q_scales = keep.tile([P, QUERIES], U8, name="q_scales", align_bytes=64)
        nc.vector.tensor_copy(out=q_bf16[:], in_=q_raw[:].rearrange("p j w -> p w j"))
        nc.vector.quantize_mx(
            out=q_words[:].bitcast(FP8X4), scales=q_scales[:], in_=q_bf16[:].rearrange("p w j -> p (w j)")
        )

        scores = []
        key_words = keep.tile([P, SLOTS], U32, name="key_words", tag="shared", align_bytes=64)
        for h in range(2):
            slots = slice(h * HALF, (h + 1) * HALF)
            entries = slice(h * HALF // LIST_ROWS, (h + 1) * HALF // LIST_ROWS)
            nc.vector.tensor_copy(key_words[:, slots], pool_words[:].indirect(offsets[:, entries]))
            bank = psum.tile([P, HALF], F32, name=f"scores{h}")
            nc.tensor.matmul_mx(
                out=bank[:],
                lhsT=q_words[:].bitcast(FP8X4),
                lhsT_scale=q_scales[:],
                rhs=key_words[:, slots].bitcast(FP8X4),
                rhs_scale=key_scales[:, slots],
                start=True,
                stop=True,
            )
            scores.append(bank)

        neg_max = keep.tile([P, 2], F32, name="neg_max")
        neg_scores = [keep.tile([P, HALF], F32, name=f"neg_scores{h}") for h in range(2)]
        for h in range(2):
            nc.vector.tensor_scalar(
                out=neg_scores[h][:], in0=scores[h][:], scalar1=-1.0, scalar2=neg_max[:, 0:1] if h else None,
                op0=ALU.mult, op1=ALU.min, accum_out=neg_max[:, h : h + 1],
            )

        exps = keep.tile([P, SLOTS], F32, name="exps")
        weighted = keep.tile([P, SLOTS], F32, name="weighted")
        exp_sums = keep.tile([P, PAGES + 1], F32, name="exp_sums")
        neg_weighted_sums = keep.tile([P, PAGES], F32, name="neg_weighted_sums")
        factor = keep.tile([P, 2], F32, name="factor")
        sum_terms = keep.tile([P, HALF_PAGES + 1], F32, name="sum_terms")

        for page in range(PAGES):
            h, j = divmod(page, HALF_PAGES)
            if page == HALF_PAGES:
                nc.scalar.activation(out=factor[:], in_=neg_max[:], func=ACT.Exp, scale=-1.0, bias=neg_max[:, 1:2])
            if page == RESCALE_BEFORE_PAGE:
                nc.scalar.activation(
                    out=sum_terms[:, :HALF_PAGES], in_=exp_sums[:, :HALF_PAGES], func=ACT.Identity,
                    scale=factor[:, 0:1], accum_out=exp_sums[:, PAGES : PAGES + 1],
                )
            nc.scalar.activation(
                out=exps[:, page * PAGE : (page + 1) * PAGE], in_=neg_scores[h][:, j * PAGE : (j + 1) * PAGE],
                func=ACT.Exp, scale=-1.0, bias=neg_max[:, h : h + 1], accum_out=exp_sums[:, page : page + 1],
            )

        neg_sum = keep.tile([P, 1], F32, name="neg_sum")
        nc.scalar.activation(
            out=sum_terms[:], in_=exp_sums[:, HALF_PAGES:], func=ACT.Identity, scale=-1.0, accum_out=neg_sum[:]
        )

        bits = neg_sum[:].bitcast(U32)
        multiples = keep.tile([P, 2], F32, name="multiples")
        nc.gpsimd.memset(multiples[:, 0:1], 2.0)
        nc.gpsimd.memset(multiples[:, 1:2], 0.5)
        steps = keep.tile([P, 10], F32, name="steps")
        exp0, bias_exp1, bias_line0, exp1, bias_line1, twice, halved, curve, line, neg_log = [
            steps[:, i : i + 1] for i in range(10)
        ]
        twice_and_halved = steps[:, 5:7]
        nc.scalar.activation(out=exp0, in_=bits, func=ACT.Exp, scale=-LN2_PER_BIT, bias=GUESS_BIAS)
        nc.scalar.activation(out=bias_exp1, in_=bits, func=ACT.Identity, scale=-LN2_PER_BIT, bias=GUESS_BIAS + 1.0)
        nc.scalar.activation(out=bias_line0, in_=bits, func=ACT.Identity, scale=-LN2_PER_BIT, bias=GUESS_BIAS + 1.25)
        nc.scalar.activation(out=twice_and_halved, in_=multiples[:], func=ACT.Identity, scale=neg_sum[:])
        nc.scalar.activation(out=exp1, in_=exp0, func=ACT.Exp, scale=neg_sum[:], bias=bias_exp1)
        nc.scalar.activation(out=bias_line1, in_=exp0, func=ACT.Identity, scale=neg_sum[:], bias=bias_line0)
        nc.scalar.activation(out=curve, in_=exp1, func=ACT.Exp, scale=twice, bias=2.0)
        nc.scalar.activation(out=line, in_=exp1, func=ACT.Identity, scale=halved, bias=bias_line1)
        nc.scalar.activation(out=neg_log, in_=curve, func=ACT.Identity, scale=0.25, bias=line)

        neg_inverse = keep.tile([P, 1], F32, name="neg_inverse")
        scaled_exp = keep.tile([P, PAGES], F32, name="scaled_exp")
        scaled_weighted = keep.tile([P, PAGES], F32, name="scaled_weighted")
        result = keep.tile([P, PAGES], F32, name="result")

        def normalise(dst, src):
            nc.vector.scalar_tensor_tensor(
                out=dst.rearrange("p (h j) -> p h j", h=2),
                in0=src.rearrange("p (h j) -> p h j", h=2),
                scalar=neg_inverse[:],
                in1=factor[:].unsqueeze(2).to_broadcast([P, 2, HALF_PAGES]),
                op0=ALU.mult,
                op1=ALU.mult,
            )

        for page in range(PAGES):
            h, j = divmod(page, HALF_PAGES)
            nc.vector.scalar_tensor_tensor(
                out=weighted[:, page * PAGE : (page + 1) * PAGE], in0=neg_scores[h][:, j * PAGE : (j + 1) * PAGE],
                scalar=neg_max[:, 1:2], in1=exps[:, page * PAGE : (page + 1) * PAGE],
                op0=ALU.subtract, op1=ALU.mult, accum_out=neg_weighted_sums[:, page : page + 1],
            )
            if page == RECIPROCAL_AFTER_PAGE:
                nc.vector.reciprocal(out=neg_inverse[:], in_=neg_sum[:])
            if page == NORMALISE_AFTER_PAGE:
                normalise(scaled_exp[:], exp_sums[:, :PAGES])
        normalise(scaled_weighted[:], neg_weighted_sums[:])
        nc.vector.scalar_tensor_tensor(
            out=result[:], in0=scaled_exp[:], scalar=neg_log, in1=scaled_weighted[:], op0=ALU.mult, op1=ALU.subtract
        )
        nc.sync.dma_start(out[0], result[:])
